import numpy as np
import ml_dtypes


def mxq(x, axis, fmt="e4m3"):
    dtype, down = {"e4m3": (ml_dtypes.float8_e4m3fn, 7), "e5m2": (ml_dtypes.float8_e5m2, 14)}[fmt]
    v = np.moveaxis(np.asarray(x, np.float32).astype(ml_dtypes.bfloat16).astype(np.float64), axis, -1)
    blocks = v.reshape(v.shape[:-1] + (-1, 32))
    amax = np.abs(blocks).max(-1, keepdims=True)
    byte = np.maximum(np.where(amax > 0, np.frexp(amax)[1] - 1 + 127, 0) - down, 1)
    scale = np.exp2(byte - 127.0)
    codes = (blocks / scale).astype(np.float32).astype(dtype).astype(np.float64)
    return np.moveaxis((codes * scale).reshape(v.shape), -1, axis)


WIDE = False


def mx_kscale(k):
    if not WIDE:
        return np.ones(k)
    levels = np.array([10, -10, 5, -5, 0])
    if k % 512:
        return np.exp2(np.random.permutation(np.resize(levels, k // 32))).repeat(32)
    a = np.empty((k // 512, 16))
    for p in range(k // 512):
        a[p, :8] = np.random.permutation(np.resize(levels, 8))
        for g in range(8):
            far = levels[np.abs(levels - a[p, g]) >= 10]
            a[p, g + 8] = far[np.random.randint(len(far))]
    return np.exp2(a.ravel()).repeat(32)


def f64(x):
    return np.asarray(x).astype(np.float64)


def striped(idx):
    return np.tile(np.asarray(idx).reshape(-1, 16).T, (8, 1)).astype(np.uint16)


def unstriped(offs):
    return offs[:16].T.reshape(-1).astype(np.int64)


E2M1 = np.array([0.0, 0.5, 1.0, 1.5, 2.0, 3.0, 4.0, 6.0, -0.0, -0.5, -1.0, -1.5, -2.0, -3.0, -4.0, -6.0])


def pack_weight(w, fmt):
    k, n = w.shape
    w = f64(np.asarray(w, np.float32).astype(ml_dtypes.bfloat16)).reshape(k // 32, 32, n)
    amax = np.abs(w).max(1)
    if fmt == "e4m3":
        byte = np.frexp(amax)[1] - 1 + 127 - 7
    else:
        mant, ex = np.frexp(amax / 6.0)
        byte = np.where(mant > 0.5, ex, ex - 1) + 127
    byte = np.clip(np.where(amax > 0, byte, 1), 1, 254)
    scaled = (w * np.exp2(127.0 - byte)[:, None, :]).reshape(k, n).astype(np.float32)
    by_word = np.ascontiguousarray(scaled.reshape(k // 512, 128, 4, n).transpose(0, 1, 3, 2))
    if fmt == "e4m3":
        words = by_word.astype(ml_dtypes.float8_e4m3fn).view(np.uint8)
    else:
        c = by_word.astype(ml_dtypes.float4_e2m1fn).view(np.uint8) & 0xF
        words = (c[..., 0::2] | (c[..., 1::2] << 4)).reshape(k // 512, 128, 2 * n)
    return np.ascontiguousarray(words), np.ascontiguousarray(byte.astype(np.uint8).reshape(k // 512, 16, n))


def unpack_weight(words, scales, fmt):
    g, _, n = scales.shape
    words = np.ascontiguousarray(words).reshape(g, 128, n, -1)
    if fmt == "e4m3":
        vals = words.view(ml_dtypes.float8_e4m3fn).astype(np.float64)
    else:
        nib = np.empty((g, 128, n, 4), np.uint8)
        nib[..., 0::2] = words & 0xF
        nib[..., 1::2] = words >> 4
        vals = E2M1[nib]
    vals = vals * np.repeat(np.exp2(scales.astype(np.float64) - 127.0), 8, axis=1)[..., None]
    return vals.transpose(0, 1, 3, 2).reshape(g * 512, n)


B, N, T, D, NQ = 1, 512, 4096, 512, 256


def setup_inputs():
    n = np.random.standard_normal
    idx = np.random.permutation(T)[:B * N]
    s = mx_kscale(D)[:, None]
    kp = pack_weight(n((D, T)) / s, "e4m3")
    return {
        "qT": (n((B, D, NQ)) * s * (1.00 / np.sqrt(D))).astype(np.float32),
        "k_words": kp[0],
        "k_scales": kp[1],
        "kb": np.tile(n(4096), (128, 1)).astype(np.float32),
        "ls": (np.random.uniform(8.5, 9.0, (B, NQ, 1))).astype(np.float32),
        "offs": striped(idx),
    }


def reference(qT, k_words, k_scales, kb, ls, offs):
    idx = unstriped(offs)
    pick = lambda x, which: x[:, which].reshape(x.shape[0], B, -1).transpose(1, 0, 2)
    k = unpack_weight(k_words, k_scales, "e4m3")
    kg = pick(k, idx)
    qq = mxq(f64(qT), 1, "e4m3")
    a = qq.transpose(0, 2, 1) @ kg
    y = a + pick(f64(kb), idx)[:, :1, :] - f64(ls)
    return y

@@ -1,0 +1,100 @@
+from contextlib import ExitStack
+
+import concourse.mybir as mybir
+from concourse.masks import make_identity
+
+F32 = mybir.dt.float32
+BF16 = mybir.dt.bfloat16
+I32 = mybir.dt.int32
+U32 = mybir.dt.uint32
+U16 = mybir.dt.uint16
+U8 = mybir.dt.uint8
+FP8X4 = mybir.dt.float8_e4m3fn_x4
+ALU = mybir.AluOpType
+
+P = 128
+T, N, D, NQ = 4096, 512, 512, 256
+PACK = 4
+PIECE = 256
+KB_ROW = P - 1
+
+FLOPS = 2 * NQ * D * N
+BYTES = P * T * 4 + 16 * T + D * NQ * 4 + T * 4 + NQ * 4 + P * (N // 16) * 2 + NQ * N * 4
+
+
+def tile_attend_logprob_topk_kernel(tc, qT, k_words, k_scales, kb, ls, offs, out):
+    nc = tc.nc
+    with ExitStack() as ctx:
+        keep = ctx.enter_context(tc.tile_pool(name="keep", bufs=1))
+        psum = ctx.enter_context(tc.psum_pool(name="psum", bufs=1))
+
+        offsets = keep.tile([P, N // 16], U16, name="offsets")
+        q_raw = keep.tile([P, PACK, NQ], F32, name="q_raw")
+        words = keep.tile([P, T], I32, name="words", align_bytes=64)
+        ls_col = keep.tile([P, NQ // P], F32, name="ls_col")
+        scale_rows = keep.tile([P, T], U8, name="scale_rows", align_bytes=64)
+        kb_row = keep.tile([P, T], F32, name="kb_row", align_bytes=64)
+        k_plane = keep.tile([P, N], U8, name="k_plane", align_bytes=64)
+        ident = keep.tile([P, P], F32, name="ident")
+
+        nc.sync.dma_start(offsets[:], offs)
+        nc.sync.dma_start(q_raw[:], qT[0].rearrange("(p t) q -> p t q", t=PACK))
+        nc.sync.dma_start(words[:], k_words[0].rearrange("p n t -> p (n t)").bitcast(I32))
+        with nc.allow_non_contiguous_dma(reason="one value a query row"):
+            nc.sync.dma_start(ls_col[:], ls[0].rearrange("(h p) o -> p (h o)", p=P))
+
+        nc.scalar.dma_start(kb_row[KB_ROW:P, :], kb[0:1, :])
+        nc.vector.memset(scale_rows[:].bitcast(I32), 0)
+        nc.scalar.dma_start(scale_rows[0:P:8, :].bitcast(I32), k_scales[0].bitcast(I32))
+        nc.vector.memset(k_plane[:].bitcast(I32), 0)
+        nc.vector.memset(kb_row[0:KB_ROW, :], 0.0)
+        make_identity(nc, ident[:])
+
+        q_bf = keep.tile([P, NQ, PACK], BF16, name="q_bf", align_bytes=64)
+        nc.scalar.copy(q_bf[:], q_raw[:].rearrange("p t q -> p q t"))
+
+        picked_scales = keep.tile([P, N], U8, name="picked_scales", align_bytes=64)
+        nc.vector.tensor_copy(picked_scales[:], scale_rows[:].indirect(offsets[:]))
+        for r in range(4):
+            nc.scalar.dma_start(k_plane[r:P:32, :].bitcast(I32), picked_scales[8 * r : P : 32, :].bitcast(I32))
+
+        picked_kb = keep.tile([P, N], F32, name="picked_kb")
+        nc.vector.tensor_copy(picked_kb[:], kb_row[:].indirect(offsets[:]))
+
+        q_codes = keep.tile([P, NQ], U32, name="q_codes", align_bytes=64)
+        q_plane = keep.tile([P, NQ], U8, name="q_plane", align_bytes=64)
+        nc.vector.quantize_mx(q_codes[:].bitcast(FP8X4), q_plane[:], q_bf[:].rearrange("p q t -> p (q t)"))
+
+        turned = psum.tile([P, N // P, P], F32, name="turned")
+        for c in range(N // P):
+            nc.tensor.transpose(turned[:, c, :], picked_kb[:, c * P : (c + 1) * P], ident[:])
+        kb_col = keep.tile([P, N // P], F32, name="kb_col")
+        nc.scalar.copy(kb_col[:], turned[:, :, KB_ROW])
+        spread = psum.tile([P, N], F32, name="spread")
+        for c in range(N // P):
+            nc.tensor.transpose(spread[:, c * P : (c + 1) * P], kb_col[:, c : c + 1].to_broadcast([P, P]), ident[:])
+        kb_all = keep.tile([P, N], F32, name="kb_all")
+        nc.scalar.copy(kb_all[:], spread[:])
+
+        k_codes = keep.tile([P, N], I32, name="k_codes", align_bytes=64)
+        nc.vector.tensor_copy(k_codes[:].bitcast(U32), words[:].bitcast(U32).indirect(offsets[:]))
+
+        for h in range(NQ // P):
+            rows = slice(h * P, (h + 1) * P)
+            for j in range(N // PIECE):
+                cols = slice(j * PIECE, (j + 1) * PIECE)
+                acc = psum.tile([P, PIECE], F32, name="acc%d%d" % (h, j))
+                nc.tensor.matmul_mx(
+                    acc[:],
+                    lhsT=q_codes[:, rows].bitcast(FP8X4),
+                    lhsT_scale=q_plane[:, rows],
+                    rhs=k_codes[:, cols].bitcast(FP8X4),
+                    rhs_scale=k_plane[:, cols],
+                    start=True,
+                    stop=True,
+                )
+                res = keep.tile([P, PIECE], F32, name="res%d%d" % (h, j))
+                nc.vector.scalar_tensor_tensor(
+                    res[:], acc[:], ls_col[:, h : h + 1], kb_all[:, cols], ALU.subtract, ALU.add
+                )
+                nc.sync.dma_start(out[0, rows, cols], res[:])

@@ -32,52 +32,69 @@ def tile_attend_logprob_topk_kernel(tc, qT, k_words, k_scales, kb, ls, offs, out
         q_raw = keep.tile([P, PACK, NQ], F32, name="q_raw")
         words = keep.tile([P, T], I32, name="words", align_bytes=64)
         ls_col = keep.tile([P, NQ // P], F32, name="ls_col")
-        scale_rows = keep.tile([P, T], U8, name="scale_rows", align_bytes=64)
-        kb_row = keep.tile([P, T], F32, name="kb_row", align_bytes=64)
+        scale_rows = keep.tile([P, T], U8, name="scale_rows", tag="slot_b", align_bytes=64)
+        kb_row = keep.tile([P, T], F32, name="kb_row", tag="slot_a", align_bytes=64)
         k_plane = keep.tile([P, N], U8, name="k_plane", align_bytes=64)
         ident = keep.tile([P, P], F32, name="ident")
 
-        nc.sync.dma_start(offsets[:], offs)
-        nc.sync.dma_start(q_raw[:], qT[0].rearrange("(p t) q -> p t q", t=PACK))
-        nc.sync.dma_start(words[:], k_words[0].rearrange("p n t -> p (n t)").bitcast(I32))
-        with nc.allow_non_contiguous_dma(reason="one value a query row"):
-            nc.sync.dma_start(ls_col[:], ls[0].rearrange("(h p) o -> p (h o)", p=P))
-
-        nc.scalar.dma_start(kb_row[KB_ROW:P, :], kb[0:1, :])
-        nc.vector.memset(scale_rows[:].bitcast(I32), 0)
-        nc.scalar.dma_start(scale_rows[0:P:8, :].bitcast(I32), k_scales[0].bitcast(I32))
-        nc.vector.memset(k_plane[:].bitcast(I32), 0)
-        nc.vector.memset(kb_row[0:KB_ROW, :], 0.0)
+        scale_words = scale_rows[:].bitcast(I32)
+        nc.vector.memset(scale_words[:, 0:255], 0)
+        nc.vector.memset(scale_words[:, 255:512], 0)
+        nc.gpsimd.memset(scale_words[:, 512:1024], 0)
+        nc.vector.memset(kb_row[0:KB_ROW, 0:1023], 0.0)
+        nc.vector.memset(kb_row[0:KB_ROW, 1023:2048], 0.0)
+        nc.gpsimd.memset(kb_row[0:KB_ROW, 2048:T], 0.0)
         make_identity(nc, ident[:])
+        nc.gpsimd.memset(k_plane[:].bitcast(I32), 0)
 
-        q_bf = keep.tile([P, NQ, PACK], BF16, name="q_bf", align_bytes=64)
-        nc.scalar.copy(q_bf[:], q_raw[:].rearrange("p t q -> p q t"))
-
-        picked_scales = keep.tile([P, N], U8, name="picked_scales", align_bytes=64)
-        nc.vector.tensor_copy(picked_scales[:], scale_rows[:].indirect(offsets[:]))
-        for r in range(4):
-            nc.scalar.dma_start(k_plane[r:P:32, :].bitcast(I32), picked_scales[8 * r : P : 32, :].bitcast(I32))
+        nc.sync.dma_start(offsets[:], offs)
+        nc.sync.dma_start(kb_row[KB_ROW:P, :], kb[0:1, :])
+        words_hbm = k_words[0].rearrange("p n t -> p (n t)").bitcast(I32)
+        nc.sync.dma_start(words[:, 0:1024], words_hbm[:, 0:1024])
+        nc.sync.dma_start(scale_rows[0:P:8, :].bitcast(I32), k_scales[0].bitcast(I32))
+        nc.sync.dma_start(words[:, 1024:T], words_hbm[:, 1024:T])
+        nc.sync.dma_start(q_raw[:], qT[0].rearrange("(p t) q -> p t q", t=PACK))
 
         picked_kb = keep.tile([P, N], F32, name="picked_kb")
         nc.vector.tensor_copy(picked_kb[:], kb_row[:].indirect(offsets[:]))
 
-        q_codes = keep.tile([P, NQ], U32, name="q_codes", align_bytes=64)
-        q_plane = keep.tile([P, NQ], U8, name="q_plane", align_bytes=64)
-        nc.vector.quantize_mx(q_codes[:].bitcast(FP8X4), q_plane[:], q_bf[:].rearrange("p q t -> p (q t)"))
+        picked_scales = keep.tile([P, N], U8, name="picked_scales", tag="slot_a", align_bytes=64)
+        nc.vector.tensor_copy(picked_scales[:], scale_rows[:].indirect(offsets[:]))
+        for r in range(4):
+            nc.sync.dma_start(k_plane[r:P:32, :].bitcast(I32), picked_scales[8 * r : P : 32, :].bitcast(I32))
+        with nc.allow_non_contiguous_dma(reason="one value a query row"):
+            nc.sync.dma_start(ls_col[:], ls[0].rearrange("(h p) o -> p (h o)", p=P))
 
-        turned = psum.tile([P, N // P, P], F32, name="turned")
-        for c in range(N // P):
-            nc.tensor.transpose(turned[:, c, :], picked_kb[:, c * P : (c + 1) * P], ident[:])
-        kb_col = keep.tile([P, N // P], F32, name="kb_col")
-        nc.scalar.copy(kb_col[:], turned[:, :, KB_ROW])
-        spread = psum.tile([P, N], F32, name="spread")
-        for c in range(N // P):
-            nc.tensor.transpose(spread[:, c * P : (c + 1) * P], kb_col[:, c : c + 1].to_broadcast([P, P]), ident[:])
-        kb_all = keep.tile([P, N], F32, name="kb_all")
-        nc.scalar.copy(kb_all[:], spread[:])
+        kb_col = []
+        for j in range(N // PIECE):
+            turned = psum.tile([P, PIECE // P, P], F32, name="turned%d" % j)
+            for c in range(PIECE // P):
+                first = j * PIECE + c * P
+                nc.tensor.transpose(turned[:, c, :], picked_kb[:, first : first + P], ident[:])
+            col = keep.tile([P, PIECE // P], F32, name="kb_col%d" % j)
+            nc.scalar.copy(col[:], turned[:, :, KB_ROW])
+            kb_col.append(col)
+        kb_all = []
+        for j in range(N // PIECE):
+            spread = psum.tile([P, PIECE], F32, name="spread%d" % j)
+            for c in range(PIECE // P):
+                nc.tensor.transpose(
+                    spread[:, c * P : (c + 1) * P], kb_col[j][:, c : c + 1].to_broadcast([P, P]), ident[:]
+                )
+            wide = keep.tile([P, PIECE], F32, name="kb_all%d" % j)
+            nc.scalar.copy(wide[:], spread[:])
+            kb_all.append(wide)
 
-        k_codes = keep.tile([P, N], I32, name="k_codes", align_bytes=64)
+        k_codes = keep.tile([P, N], I32, name="k_codes", tag="slot_b", align_bytes=64)
         nc.vector.tensor_copy(k_codes[:].bitcast(U32), words[:].bitcast(U32).indirect(offsets[:]))
+
+        q_bf = [keep.tile([P, P, PACK], BF16, name="q_bf%d" % h, align_bytes=64) for h in range(2)]
+        q_codes = [keep.tile([P, P], U32, name="q_codes%d" % h, align_bytes=64) for h in range(2)]
+        q_plane = [keep.tile([P, P], U8, name="q_plane%d" % h, align_bytes=64) for h in range(2)]
+        nc.vector.tensor_copy(q_bf[0][:], q_raw[:, :, 0:P].rearrange("p t q -> p q t"))
+        nc.scalar.copy(q_bf[1][:], q_raw[:, :, P:NQ].rearrange("p t q -> p q t"))
+        for h in range(2):
+            nc.vector.quantize_mx(q_codes[h][:].bitcast(FP8X4), q_plane[h][:], q_bf[h][:].rearrange("p q t -> p (q t)"))
 
         for h in range(NQ // P):
             rows = slice(h * P, (h + 1) * P)
@@ -86,8 +103,8 @@ def tile_attend_logprob_topk_kernel(tc, qT, k_words, k_scales, kb, ls, offs, out
                 acc = psum.tile([P, PIECE], F32, name="acc%d%d" % (h, j))
                 nc.tensor.matmul_mx(
                     acc[:],
-                    lhsT=q_codes[:, rows].bitcast(FP8X4),
-                    lhsT_scale=q_plane[:, rows],
+                    lhsT=q_codes[h][:].bitcast(FP8X4),
+                    lhsT_scale=q_plane[h][:],
                     rhs=k_codes[:, cols].bitcast(FP8X4),
                     rhs_scale=k_plane[:, cols],
                     start=True,
@@ -95,6 +112,6 @@ def tile_attend_logprob_topk_kernel(tc, qT, k_words, k_scales, kb, ls, offs, out
                 )
                 res = keep.tile([P, PIECE], F32, name="res%d%d" % (h, j))
                 nc.vector.scalar_tensor_tensor(
-                    res[:], acc[:], ls_col[:, h : h + 1], kb_all[:, cols], ALU.subtract, ALU.add
+                    res[:], acc[:], ls_col[:, h : h + 1], kb_all[j][:], ALU.subtract, ALU.add
                 )
                 nc.sync.dma_start(out[0, rows, cols], res[:])

@@ -17,6 +17,7 @@ T, N, D, NQ = 4096, 512, 512, 256
 PACK = 4
 PIECE = 256
 KB_ROW = P - 1
+HEAD = 512
 
 FLOPS = 2 * NQ * D * N
 BYTES = P * T * 4 + 16 * T + D * NQ * 4 + T * 4 + NQ * 4 + P * (N // 16) * 2 + NQ * N * 4
@@ -46,13 +47,16 @@ def tile_attend_logprob_topk_kernel(tc, qT, k_words, k_scales, kb, ls, offs, out
         nc.gpsimd.memset(kb_row[0:KB_ROW, 2048:T], 0.0)
         make_identity(nc, ident[:])
         nc.gpsimd.memset(k_plane[:].bitcast(I32), 0)
+        ls_rows = keep.tile([P, P], F32, name="ls_rows")
+        nc.gpsimd.memset(ls_rows[0 : P - 2, :], 0.0)
 
-        nc.sync.dma_start(offsets[:], offs)
-        nc.sync.dma_start(kb_row[KB_ROW:P, :], kb[0:1, :])
         words_hbm = k_words[0].rearrange("p n t -> p (n t)").bitcast(I32)
-        nc.sync.dma_start(words[:, 0:1024], words_hbm[:, 0:1024])
+        nc.sync.dma_start(words[:, 0:HEAD], words_hbm[:, 0:HEAD])
+        nc.sync.dma_start(kb_row[KB_ROW:P, :], kb[0:1, :])
+        nc.sync.dma_start(offsets[:], offs)
+        nc.sync.dma_start(ls_rows[P - 2 : P, :], ls[0].rearrange("(h p) o -> h (p o)", p=P))
         nc.sync.dma_start(scale_rows[0:P:8, :].bitcast(I32), k_scales[0].bitcast(I32))
-        nc.sync.dma_start(words[:, 1024:T], words_hbm[:, 1024:T])
+        nc.sync.dma_start(words[:, HEAD:T], words_hbm[:, HEAD:T])
         nc.sync.dma_start(q_raw[:], qT[0].rearrange("(p t) q -> p t q", t=PACK))
 
         picked_kb = keep.tile([P, N], F32, name="picked_kb")
@@ -62,8 +66,10 @@ def tile_attend_logprob_topk_kernel(tc, qT, k_words, k_scales, kb, ls, offs, out
         nc.vector.tensor_copy(picked_scales[:], scale_rows[:].indirect(offsets[:]))
         for r in range(4):
             nc.sync.dma_start(k_plane[r:P:32, :].bitcast(I32), picked_scales[8 * r : P : 32, :].bitcast(I32))
-        with nc.allow_non_contiguous_dma(reason="one value a query row"):
-            nc.sync.dma_start(ls_col[:], ls[0].rearrange("(h p) o -> p (h o)", p=P))
+
+        ls_turned = psum.tile([P, P], F32, name="ls_turned", tag="last_bank")
+        nc.tensor.transpose(ls_turned[:], ls_rows[:], ident[:])
+        nc.scalar.copy(ls_col[:], ls_turned[:, P - 2 : P])
 
         kb_col = []
         for j in range(N // PIECE):
@@ -100,7 +106,7 @@ def tile_attend_logprob_topk_kernel(tc, qT, k_words, k_scales, kb, ls, offs, out
             rows = slice(h * P, (h + 1) * P)
             for j in range(N // PIECE):
                 cols = slice(j * PIECE, (j + 1) * PIECE)
-                acc = psum.tile([P, PIECE], F32, name="acc%d%d" % (h, j))
+                acc = psum.tile([P, PIECE], F32, name="acc%d%d" % (h, j), tag="last_bank" if h + j == 2 else "acc%d%d" % (h, j))
                 nc.tensor.matmul_mx(
                     acc[:],
                     lhsT=q_codes[h][:].bitcast(FP8X4),

@@ -17,7 +17,8 @@ T, N, D, NQ = 4096, 512, 512, 256
 PACK = 4
 PIECE = 256
 KB_ROW = P - 1
-HEAD = 512
+HEAD = 896
+SPLIT = 80
 
 FLOPS = 2 * NQ * D * N
 BYTES = P * T * 4 + 16 * T + D * NQ * 4 + T * 4 + NQ * 4 + P * (N // 16) * 2 + NQ * N * 4
@@ -30,8 +31,7 @@ def tile_attend_logprob_topk_kernel(tc, qT, k_words, k_scales, kb, ls, offs, out
         psum = ctx.enter_context(tc.psum_pool(name="psum", bufs=1))
 
         offsets = keep.tile([P, N // 16], U16, name="offsets")
-        q_raw = keep.tile([P, PACK, NQ], F32, name="q_raw")
-        words = keep.tile([P, T], I32, name="words", align_bytes=64)
+        words = keep.tile([P, T], I32, name="words", tag="slot_w", align_bytes=64)
         ls_col = keep.tile([P, NQ // P], F32, name="ls_col")
         scale_rows = keep.tile([P, T], U8, name="scale_rows", tag="slot_b", align_bytes=64)
         kb_row = keep.tile([P, T], F32, name="kb_row", tag="slot_a", align_bytes=64)
@@ -42,34 +42,52 @@ def tile_attend_logprob_topk_kernel(tc, qT, k_words, k_scales, kb, ls, offs, out
         nc.vector.memset(scale_words[:, 0:255], 0)
         nc.vector.memset(scale_words[:, 255:512], 0)
         nc.gpsimd.memset(scale_words[:, 512:1024], 0)
-        nc.vector.memset(kb_row[0:KB_ROW, 0:1023], 0.0)
-        nc.vector.memset(kb_row[0:KB_ROW, 1023:2048], 0.0)
-        nc.gpsimd.memset(kb_row[0:KB_ROW, 2048:T], 0.0)
-        make_identity(nc, ident[:])
-        nc.gpsimd.memset(k_plane[:].bitcast(I32), 0)
+        nc.vector.memset(kb_row[0:KB_ROW, 0:895], 0.0)
+        nc.vector.memset(kb_row[0:KB_ROW, 895:1792], 0.0)
         ls_rows = keep.tile([P, P], F32, name="ls_rows")
         nc.gpsimd.memset(ls_rows[0 : P - 2, :], 0.0)
+        make_identity(nc, ident[:])
+        nc.gpsimd.memset(k_plane[:].bitcast(I32), 0)
+        nc.gpsimd.memset(kb_row[0:KB_ROW, 1792:T], 0.0)
 
         words_hbm = k_words[0].rearrange("p n t -> p (n t)").bitcast(I32)
+        q_hbm = qT[0].rearrange("(p t) q -> p t q", t=PACK)
         nc.sync.dma_start(words[:, 0:HEAD], words_hbm[:, 0:HEAD])
-        nc.sync.dma_start(kb_row[KB_ROW:P, :], kb[0:1, :])
-        nc.sync.dma_start(offsets[:], offs)
         nc.sync.dma_start(ls_rows[P - 2 : P, :], ls[0].rearrange("(h p) o -> h (p o)", p=P))
+        nc.sync.dma_start(offsets[:], offs)
         nc.sync.dma_start(scale_rows[0:P:8, :].bitcast(I32), k_scales[0].bitcast(I32))
+        nc.sync.dma_start(kb_row[KB_ROW:P, :], kb[0:1, :])
         nc.sync.dma_start(words[:, HEAD:T], words_hbm[:, HEAD:T])
-        nc.sync.dma_start(q_raw[:], qT[0].rearrange("(p t) q -> p t q", t=PACK))
-
-        picked_kb = keep.tile([P, N], F32, name="picked_kb")
-        nc.vector.tensor_copy(picked_kb[:], kb_row[:].indirect(offsets[:]))
-
-        picked_scales = keep.tile([P, N], U8, name="picked_scales", tag="slot_a", align_bytes=64)
-        nc.vector.tensor_copy(picked_scales[:], scale_rows[:].indirect(offsets[:]))
-        for r in range(4):
-            nc.sync.dma_start(k_plane[r:P:32, :].bitcast(I32), picked_scales[8 * r : P : 32, :].bitcast(I32))
+        q_raw0 = keep.tile([P, PACK, P], F32, name="q_raw0", tag="slot_c")
+        nc.sync.dma_start(q_raw0[:], q_hbm[:, :, 0:P])
 
         ls_turned = psum.tile([P, P], F32, name="ls_turned", tag="last_bank")
         nc.tensor.transpose(ls_turned[:], ls_rows[:], ident[:])
         nc.scalar.copy(ls_col[:], ls_turned[:, P - 2 : P])
+
+        picked_scales = keep.tile([P, N], U8, name="picked_scales", align_bytes=64)
+        nc.vector.tensor_copy(picked_scales[:], scale_rows[:].indirect(offsets[:]))
+        for r in range(4):
+            nc.sync.dma_start(k_plane[r:P:32, :].bitcast(I32), picked_scales[8 * r : P : 32, :].bitcast(I32))
+        q_raw1 = keep.tile([P, PACK, P], F32, name="q_raw1", tag="slot_b", align_bytes=64)
+        nc.sync.dma_start(q_raw1[:], q_hbm[:, :, P:NQ])
+
+        picked_kb = keep.tile([P, N], F32, name="picked_kb")
+        nc.vector.tensor_copy(picked_kb[:], kb_row[:].indirect(offsets[:]))
+
+        q_codes = [keep.tile([P, P], U32, name="q_codes%d" % h, align_bytes=64) for h in range(2)]
+        q_plane = [keep.tile([P, P], U8, name="q_plane%d" % h, align_bytes=64) for h in range(2)]
+
+        q_bf = [keep.tile([P, P, PACK], BF16, name="q_bf0", align_bytes=64)]
+
+        def cast_views(h, raw, first, last):
+            return (
+                q_bf[h][:, first:last, :].rearrange("p (c i) t -> p c t i", i=4),
+                raw[:, :, first:last].rearrange("p t (c i) -> p c t i", i=4),
+            )
+
+        def quantise_queries(h):
+            nc.vector.quantize_mx(q_codes[h][:].bitcast(FP8X4), q_plane[h][:], q_bf[h][:].rearrange("p q t -> p (q t)"))
 
         kb_col = []
         for j in range(N // PIECE):
@@ -80,30 +98,32 @@ def tile_attend_logprob_topk_kernel(tc, qT, k_words, k_scales, kb, ls, offs, out
             col = keep.tile([P, PIECE // P], F32, name="kb_col%d" % j)
             nc.scalar.copy(col[:], turned[:, :, KB_ROW])
             kb_col.append(col)
-        kb_all = []
+        spreads = []
         for j in range(N // PIECE):
             spread = psum.tile([P, PIECE], F32, name="spread%d" % j)
             for c in range(PIECE // P):
                 nc.tensor.transpose(
                     spread[:, c * P : (c + 1) * P], kb_col[j][:, c : c + 1].to_broadcast([P, P]), ident[:]
                 )
-            wide = keep.tile([P, PIECE], F32, name="kb_all%d" % j)
-            nc.scalar.copy(wide[:], spread[:])
-            kb_all.append(wide)
+            spreads.append(spread)
 
-        k_codes = keep.tile([P, N], I32, name="k_codes", tag="slot_b", align_bytes=64)
+        k_codes = keep.tile([P, N], I32, name="k_codes", tag="slot_a", align_bytes=64)
         nc.vector.tensor_copy(k_codes[:].bitcast(U32), words[:].bitcast(U32).indirect(offsets[:]))
 
-        q_bf = [keep.tile([P, P, PACK], BF16, name="q_bf%d" % h, align_bytes=64) for h in range(2)]
-        q_codes = [keep.tile([P, P], U32, name="q_codes%d" % h, align_bytes=64) for h in range(2)]
-        q_plane = [keep.tile([P, P], U8, name="q_plane%d" % h, align_bytes=64) for h in range(2)]
-        nc.vector.tensor_copy(q_bf[0][:], q_raw[:, :, 0:P].rearrange("p t q -> p q t"))
-        nc.scalar.copy(q_bf[1][:], q_raw[:, :, P:NQ].rearrange("p t q -> p q t"))
-        for h in range(2):
-            nc.vector.quantize_mx(q_codes[h][:].bitcast(FP8X4), q_plane[h][:], q_bf[h][:].rearrange("p q t -> p (q t)"))
+        nc.scalar.copy(*cast_views(0, q_raw0, 0, P))
+        quantise_queries(0)
+        kb_all = [keep.tile([P, PIECE], F32, name="kb_all0", tag="slot_c")]
+        nc.scalar.copy(kb_all[0][:], spreads[0][:])
+        q_bf.append(keep.tile([P, P, PACK], BF16, name="q_bf1", tag="slot_w", align_bytes=64))
+        nc.vector.tensor_copy(*cast_views(1, q_raw1, 0, SPLIT))
+        nc.scalar.copy(*cast_views(1, q_raw1, SPLIT, P))
+        kb_all.append(keep.tile([P, PIECE], F32, name="kb_all1", tag="slot_b", align_bytes=64))
+        nc.scalar.copy(kb_all[1][:], spreads[1][:])
+        quantise_queries(1)
 
         for h in range(NQ // P):
             rows = slice(h * P, (h + 1) * P)
+            res = keep.tile([P, N], F32, name="res%d" % h, tag="slot_w" if h == 0 else "res1", align_bytes=64)
             for j in range(N // PIECE):
                 cols = slice(j * PIECE, (j + 1) * PIECE)
                 acc = psum.tile([P, PIECE], F32, name="acc%d%d" % (h, j), tag="last_bank" if h + j == 2 else "acc%d%d" % (h, j))
@@ -116,8 +136,7 @@ def tile_attend_logprob_topk_kernel(tc, qT, k_words, k_scales, kb, ls, offs, out
                     start=True,
                     stop=True,
                 )
-                res = keep.tile([P, PIECE], F32, name="res%d%d" % (h, j))
                 nc.vector.scalar_tensor_tensor(
-                    res[:], acc[:], ls_col[:, h : h + 1], kb_all[j][:], ALU.subtract, ALU.add
+                    res[:, cols], acc[:], ls_col[:, h : h + 1], kb_all[j][:], ALU.subtract, ALU.add
                 )
-                nc.sync.dma_start(out[0, rows, cols], res[:])
+                nc.sync.dma_start(out[0, rows, cols], res[:, cols])

@@ -18,7 +18,7 @@ PACK = 4
 PIECE = 256
 KB_ROW = P - 1
 HEAD = 896
-SPLIT = 80
+SPLIT0 = 96
 
 FLOPS = 2 * NQ * D * N
 BYTES = P * T * 4 + 16 * T + D * NQ * 4 + T * 4 + NQ * 4 + P * (N // 16) * 2 + NQ * N * 4
@@ -110,20 +110,22 @@ def tile_attend_logprob_topk_kernel(tc, qT, k_words, k_scales, kb, ls, offs, out
         k_codes = keep.tile([P, N], I32, name="k_codes", tag="slot_a", align_bytes=64)
         nc.vector.tensor_copy(k_codes[:].bitcast(U32), words[:].bitcast(U32).indirect(offsets[:]))
 
-        nc.scalar.copy(*cast_views(0, q_raw0, 0, P))
+        nc.scalar.copy(*cast_views(0, q_raw0, 0, SPLIT0))
+        nc.gpsimd.tensor_scalar(
+            q_bf[0][:, SPLIT0:P, :], q_raw0[:, :, SPLIT0:P].rearrange("p t q -> p q t"), 1.0, 0.0, ALU.mult, ALU.add
+        )
         quantise_queries(0)
         kb_all = [keep.tile([P, PIECE], F32, name="kb_all0", tag="slot_c")]
-        nc.scalar.copy(kb_all[0][:], spreads[0][:])
-        q_bf.append(keep.tile([P, P, PACK], BF16, name="q_bf1", tag="slot_w", align_bytes=64))
-        nc.vector.tensor_copy(*cast_views(1, q_raw1, 0, SPLIT))
-        nc.scalar.copy(*cast_views(1, q_raw1, SPLIT, P))
+        q_bf.append(keep.tile([P, P, PACK], BF16, name="q_bf1", tag="slot_d", align_bytes=64))
+        nc.scalar.copy(*cast_views(1, q_raw1, 0, P))
+        nc.vector.tensor_copy(kb_all[0][:], spreads[0][:])
         kb_all.append(keep.tile([P, PIECE], F32, name="kb_all1", tag="slot_b", align_bytes=64))
         nc.scalar.copy(kb_all[1][:], spreads[1][:])
         quantise_queries(1)
 
         for h in range(NQ // P):
             rows = slice(h * P, (h + 1) * P)
-            res = keep.tile([P, N], F32, name="res%d" % h, tag="slot_w" if h == 0 else "res1", align_bytes=64)
+            res = keep.tile([P, N], F32, name="res%d" % h, tag="slot_d" if h == 0 else "res1", align_bytes=64)
             for j in range(N // PIECE):
                 cols = slice(j * PIECE, (j + 1) * PIECE)
                 acc = psum.tile([P, PIECE], F32, name="acc%d%d" % (h, j), tag="last_bank" if h + j == 2 else "acc%d%d" % (h, j))

@@ -17,8 +17,6 @@ T, N, D, NQ = 4096, 512, 512, 256
 PACK = 4
 PIECE = 256
 KB_ROW = P - 1
-HEAD = 896
-SPLIT0 = 96
 
 FLOPS = 2 * NQ * D * N
 BYTES = P * T * 4 + 16 * T + D * NQ * 4 + T * 4 + NQ * 4 + P * (N // 16) * 2 + NQ * N * 4
@@ -31,12 +29,13 @@ def tile_attend_logprob_topk_kernel(tc, qT, k_words, k_scales, kb, ls, offs, out
         psum = ctx.enter_context(tc.psum_pool(name="psum", bufs=1))
 
         offsets = keep.tile([P, N // 16], U16, name="offsets")
-        words = keep.tile([P, T], I32, name="words", tag="slot_w", align_bytes=64)
+        words = keep.tile([P, T], I32, name="words", align_bytes=64)
         ls_col = keep.tile([P, NQ // P], F32, name="ls_col")
-        scale_rows = keep.tile([P, T], U8, name="scale_rows", tag="slot_b", align_bytes=64)
-        kb_row = keep.tile([P, T], F32, name="kb_row", tag="slot_a", align_bytes=64)
+        scale_rows = keep.tile([P, T], U8, name="scale_rows", align_bytes=64)
+        kb_row = keep.tile([P, T], F32, name="kb_row", tag="kb_then_codes", align_bytes=64)
         k_plane = keep.tile([P, N], U8, name="k_plane", align_bytes=64)
         ident = keep.tile([P, P], F32, name="ident")
+        q_raw = keep.tile([P, PACK, NQ], F32, name="q_raw")
 
         scale_words = scale_rows[:].bitcast(I32)
         nc.vector.memset(scale_words[:, 0:255], 0)
@@ -51,94 +50,75 @@ def tile_attend_logprob_topk_kernel(tc, qT, k_words, k_scales, kb, ls, offs, out
         nc.gpsimd.memset(kb_row[0:KB_ROW, 1792:T], 0.0)
 
         words_hbm = k_words[0].rearrange("p n t -> p (n t)").bitcast(I32)
-        q_hbm = qT[0].rearrange("(p t) q -> p t q", t=PACK)
-        nc.sync.dma_start(words[:, 0:HEAD], words_hbm[:, 0:HEAD])
+        nc.sync.dma_start(q_raw[:], qT[0].rearrange("(p t) q -> p t q", t=PACK))
+        nc.sync.dma_start(kb_row[KB_ROW:P, :], kb[0:1, :])
         nc.sync.dma_start(ls_rows[P - 2 : P, :], ls[0].rearrange("(h p) o -> h (p o)", p=P))
         nc.sync.dma_start(offsets[:], offs)
         nc.sync.dma_start(scale_rows[0:P:8, :].bitcast(I32), k_scales[0].bitcast(I32))
-        nc.sync.dma_start(kb_row[KB_ROW:P, :], kb[0:1, :])
-        nc.sync.dma_start(words[:, HEAD:T], words_hbm[:, HEAD:T])
-        q_raw0 = keep.tile([P, PACK, P], F32, name="q_raw0", tag="slot_c")
-        nc.sync.dma_start(q_raw0[:], q_hbm[:, :, 0:P])
+        nc.sync.dma_start(words[:], words_hbm)
 
-        ls_turned = psum.tile([P, P], F32, name="ls_turned", tag="last_bank")
+        ls_turned = psum.tile([P, P], F32, name="ls_turned")
         nc.tensor.transpose(ls_turned[:], ls_rows[:], ident[:])
         nc.scalar.copy(ls_col[:], ls_turned[:, P - 2 : P])
+
+        q_bf = keep.tile([P, NQ, PACK], BF16, name="q_bf", align_bytes=64)
+        nc.scalar.copy(
+            q_bf[:].rearrange("p (c i) t -> p c t i", i=4),
+            q_raw[:].rearrange("p t (c i) -> p c t i", i=4),
+        )
 
         picked_scales = keep.tile([P, N], U8, name="picked_scales", align_bytes=64)
         nc.vector.tensor_copy(picked_scales[:], scale_rows[:].indirect(offsets[:]))
         for r in range(4):
-            nc.sync.dma_start(k_plane[r:P:32, :].bitcast(I32), picked_scales[8 * r : P : 32, :].bitcast(I32))
-        q_raw1 = keep.tile([P, PACK, P], F32, name="q_raw1", tag="slot_b", align_bytes=64)
-        nc.sync.dma_start(q_raw1[:], q_hbm[:, :, P:NQ])
+            nc.scalar.dma_start(k_plane[r:P:32, :].bitcast(I32), picked_scales[8 * r : P : 32, :].bitcast(I32))
 
-        picked_kb = keep.tile([P, N], F32, name="picked_kb")
-        nc.vector.tensor_copy(picked_kb[:], kb_row[:].indirect(offsets[:]))
-
-        q_codes = [keep.tile([P, P], U32, name="q_codes%d" % h, align_bytes=64) for h in range(2)]
-        q_plane = [keep.tile([P, P], U8, name="q_plane%d" % h, align_bytes=64) for h in range(2)]
-
-        q_bf = [keep.tile([P, P, PACK], BF16, name="q_bf0", align_bytes=64)]
-
-        def cast_views(h, raw, first, last):
-            return (
-                q_bf[h][:, first:last, :].rearrange("p (c i) t -> p c t i", i=4),
-                raw[:, :, first:last].rearrange("p t (c i) -> p c t i", i=4),
-            )
-
-        def quantise_queries(h):
-            nc.vector.quantize_mx(q_codes[h][:].bitcast(FP8X4), q_plane[h][:], q_bf[h][:].rearrange("p q t -> p (q t)"))
-
-        kb_col = []
+        listed = [offsets[:, j * PIECE // 16 : (j + 1) * PIECE // 16] for j in range(N // PIECE)]
+        picked_kb = []
         for j in range(N // PIECE):
-            turned = psum.tile([P, PIECE // P, P], F32, name="turned%d" % j)
+            picked = keep.tile([P, PIECE], F32, name="picked_kb%d" % j)
+            nc.vector.tensor_copy(picked[:], kb_row[:].indirect(listed[j]))
+            picked_kb.append(picked)
+
+        q_codes = keep.tile([P, NQ], U32, name="q_codes", tag="kb_then_codes", align_bytes=64)
+        q_plane = keep.tile([P, NQ], U8, name="q_plane", align_bytes=64)
+        nc.vector.quantize_mx(q_codes[:].bitcast(FP8X4), q_plane[:], q_bf[:].rearrange("p q t -> p (q t)"))
+
+        kb_all = []
+        for j in range(N // PIECE):
+            turned = psum.tile([P, PIECE // P, P], F32, name="turned%d" % j, tag="ls_turned" if j else "turned")
             for c in range(PIECE // P):
-                first = j * PIECE + c * P
-                nc.tensor.transpose(turned[:, c, :], picked_kb[:, first : first + P], ident[:])
+                nc.tensor.transpose(turned[:, c, :], picked_kb[j][:, c * P : (c + 1) * P], ident[:])
             col = keep.tile([P, PIECE // P], F32, name="kb_col%d" % j)
             nc.scalar.copy(col[:], turned[:, :, KB_ROW])
-            kb_col.append(col)
-        spreads = []
-        for j in range(N // PIECE):
             spread = psum.tile([P, PIECE], F32, name="spread%d" % j)
             for c in range(PIECE // P):
-                nc.tensor.transpose(
-                    spread[:, c * P : (c + 1) * P], kb_col[j][:, c : c + 1].to_broadcast([P, P]), ident[:]
-                )
-            spreads.append(spread)
+                nc.tensor.transpose(spread[:, c * P : (c + 1) * P], col[:, c : c + 1].to_broadcast([P, P]), ident[:])
+            spread_sb = keep.tile([P, PIECE], F32, name="kb_all%d" % j)
+            nc.scalar.copy(spread_sb[:], spread[:])
+            kb_all.append(spread_sb)
 
-        k_codes = keep.tile([P, N], I32, name="k_codes", tag="slot_a", align_bytes=64)
-        nc.vector.tensor_copy(k_codes[:].bitcast(U32), words[:].bitcast(U32).indirect(offsets[:]))
+        k_codes = []
+        for j in range(N // PIECE):
+            codes = keep.tile([P, PIECE], U32, name="k_codes%d" % j, align_bytes=64)
+            nc.vector.tensor_copy(codes[:], words[:].bitcast(U32).indirect(listed[j]))
+            k_codes.append(codes)
 
-        nc.scalar.copy(*cast_views(0, q_raw0, 0, SPLIT0))
-        nc.gpsimd.tensor_scalar(
-            q_bf[0][:, SPLIT0:P, :], q_raw0[:, :, SPLIT0:P].rearrange("p t q -> p q t"), 1.0, 0.0, ALU.mult, ALU.add
-        )
-        quantise_queries(0)
-        kb_all = [keep.tile([P, PIECE], F32, name="kb_all0", tag="slot_c")]
-        q_bf.append(keep.tile([P, P, PACK], BF16, name="q_bf1", tag="slot_d", align_bytes=64))
-        nc.scalar.copy(*cast_views(1, q_raw1, 0, P))
-        nc.vector.tensor_copy(kb_all[0][:], spreads[0][:])
-        kb_all.append(keep.tile([P, PIECE], F32, name="kb_all1", tag="slot_b", align_bytes=64))
-        nc.scalar.copy(kb_all[1][:], spreads[1][:])
-        quantise_queries(1)
-
-        for h in range(NQ // P):
-            rows = slice(h * P, (h + 1) * P)
-            res = keep.tile([P, N], F32, name="res%d" % h, tag="slot_d" if h == 0 else "res1", align_bytes=64)
-            for j in range(N // PIECE):
-                cols = slice(j * PIECE, (j + 1) * PIECE)
-                acc = psum.tile([P, PIECE], F32, name="acc%d%d" % (h, j), tag="last_bank" if h + j == 2 else "acc%d%d" % (h, j))
+        for j in range(N // PIECE):
+            cols = slice(j * PIECE, (j + 1) * PIECE)
+            for h in range(NQ // P):
+                rows = slice(h * P, (h + 1) * P)
+                acc = psum.tile([P, PIECE], F32, name="acc%d%d" % (h, j))
                 nc.tensor.matmul_mx(
                     acc[:],
-                    lhsT=q_codes[h][:].bitcast(FP8X4),
-                    lhsT_scale=q_plane[h][:],
-                    rhs=k_codes[:, cols].bitcast(FP8X4),
+                    lhsT=q_codes[:, rows].bitcast(FP8X4),
+                    lhsT_scale=q_plane[:, rows],
+                    rhs=k_codes[j][:].bitcast(FP8X4),
                     rhs_scale=k_plane[:, cols],
                     start=True,
                     stop=True,
                 )
+                res = keep.tile([P, PIECE], F32, name="res%d%d" % (h, j))
                 nc.vector.scalar_tensor_tensor(
-                    res[:, cols], acc[:], ls_col[:, h : h + 1], kb_all[j][:], ALU.subtract, ALU.add
+                    res[:], acc[:], ls_col[:, h : h + 1], kb_all[j][:], ALU.subtract, ALU.add
                 )
-                nc.sync.dma_start(out[0, rows, cols], res[:, cols])
+                nc.sync.dma_start(out[0, rows, cols], res[:])

@@ -51,10 +51,10 @@ def tile_attend_logprob_topk_kernel(tc, qT, k_words, k_scales, kb, ls, offs, out
 
         words_hbm = k_words[0].rearrange("p n t -> p (n t)").bitcast(I32)
         nc.sync.dma_start(q_raw[:], qT[0].rearrange("(p t) q -> p t q", t=PACK))
-        nc.sync.dma_start(kb_row[KB_ROW:P, :], kb[0:1, :])
         nc.sync.dma_start(ls_rows[P - 2 : P, :], ls[0].rearrange("(h p) o -> h (p o)", p=P))
         nc.sync.dma_start(offsets[:], offs)
         nc.sync.dma_start(scale_rows[0:P:8, :].bitcast(I32), k_scales[0].bitcast(I32))
+        nc.sync.dma_start(kb_row[KB_ROW:P, :], kb[0:1, :])
         nc.sync.dma_start(words[:], words_hbm)
 
         ls_turned = psum.tile([P, P], F32, name="ls_turned")
@@ -70,7 +70,7 @@ def tile_attend_logprob_topk_kernel(tc, qT, k_words, k_scales, kb, ls, offs, out
         picked_scales = keep.tile([P, N], U8, name="picked_scales", align_bytes=64)
         nc.vector.tensor_copy(picked_scales[:], scale_rows[:].indirect(offsets[:]))
         for r in range(4):
-            nc.scalar.dma_start(k_plane[r:P:32, :].bitcast(I32), picked_scales[8 * r : P : 32, :].bitcast(I32))
+            nc.sync.dma_start(k_plane[r:P:32, :].bitcast(I32), picked_scales[8 * r : P : 32, :].bitcast(I32))
 
         listed = [offsets[:, j * PIECE // 16 : (j + 1) * PIECE // 16] for j in range(N // PIECE)]
         picked_kb = []

@@ -11,12 +11,14 @@ U16 = mybir.dt.uint16
 U8 = mybir.dt.uint8
 FP8X4 = mybir.dt.float8_e4m3fn_x4
 ALU = mybir.AluOpType
+COPY = mybir.ActivationFunctionType.Copy
 
 P = 128
 T, N, D, NQ = 4096, 512, 512, 256
 PACK = 4
 PIECE = 256
-KB_ROW = P - 1
+KB_ROWS = (P - 1, P // 2 - 1)
+HALF = T // 2
 
 FLOPS = 2 * NQ * D * N
 BYTES = P * T * 4 + 16 * T + D * NQ * 4 + T * 4 + NQ * 4 + P * (N // 16) * 2 + NQ * N * 4
@@ -40,21 +42,26 @@ def tile_attend_logprob_topk_kernel(tc, qT, k_words, k_scales, kb, ls, offs, out
         scale_words = scale_rows[:].bitcast(I32)
         nc.vector.memset(scale_words[:, 0:255], 0)
         nc.vector.memset(scale_words[:, 255:512], 0)
+        nc.gpsimd.memset(ident[:], 0.0)
         nc.gpsimd.memset(scale_words[:, 512:1024], 0)
-        nc.vector.memset(kb_row[0:KB_ROW, 0:895], 0.0)
-        nc.vector.memset(kb_row[0:KB_ROW, 895:1792], 0.0)
+        nc.vector.memset(kb_row[0 : KB_ROWS[0], 0:1023], 0.0)
+        nc.vector.memset(kb_row[0 : KB_ROWS[0], 1023:HALF], 0.0)
+        nc.vector.memset(kb_row[0 : KB_ROWS[1], HALF : HALF + 575], 0.0)
+        nc.vector.memset(kb_row[0 : KB_ROWS[1], HALF + 575 : HALF + 1152], 0.0)
         ls_rows = keep.tile([P, P], F32, name="ls_rows")
         nc.gpsimd.memset(ls_rows[0 : P - 2, :], 0.0)
-        make_identity(nc, ident[:])
-        nc.gpsimd.memset(k_plane[:].bitcast(I32), 0)
-        nc.gpsimd.memset(kb_row[0:KB_ROW, 1792:T], 0.0)
+        make_identity(nc, ident[:], nomemset=True)
+        nc.gpsimd.memset(kb_row[0 : KB_ROWS[1], HALF + 1152 : T], 0.0)
+        nc.gpsimd.memset(kb_row[P // 2 : P, HALF:T], 0.0)
 
         words_hbm = k_words[0].rearrange("p n t -> p (n t)").bitcast(I32)
         nc.sync.dma_start(q_raw[:], qT[0].rearrange("(p t) q -> p t q", t=PACK))
         nc.sync.dma_start(ls_rows[P - 2 : P, :], ls[0].rearrange("(h p) o -> h (p o)", p=P))
         nc.sync.dma_start(offsets[:], offs)
         nc.sync.dma_start(scale_rows[0:P:8, :].bitcast(I32), k_scales[0].bitcast(I32))
-        nc.sync.dma_start(kb_row[KB_ROW:P, :], kb[0:1, :])
+        for half, row in enumerate(KB_ROWS):
+            stretch = slice(half * HALF, (half + 1) * HALF)
+            nc.sync.dma_start(kb_row[row : row + 1, stretch], kb[0:1, stretch])
         nc.sync.dma_start(words[:], words_hbm)
 
         ls_turned = psum.tile([P, P], F32, name="ls_turned")
@@ -69,14 +76,15 @@ def tile_attend_logprob_topk_kernel(tc, qT, k_words, k_scales, kb, ls, offs, out
 
         picked_scales = keep.tile([P, N], U8, name="picked_scales", align_bytes=64)
         nc.vector.tensor_copy(picked_scales[:], scale_rows[:].indirect(offsets[:]))
-        for r in range(4):
+        nc.vector.tensor_copy(k_plane[:].bitcast(I32), picked_scales[:].bitcast(I32))
+        for r in range(1, 4):
             nc.sync.dma_start(k_plane[r:P:32, :].bitcast(I32), picked_scales[8 * r : P : 32, :].bitcast(I32))
 
         listed = [offsets[:, j * PIECE // 16 : (j + 1) * PIECE // 16] for j in range(N // PIECE)]
         picked_kb = []
         for j in range(N // PIECE):
             picked = keep.tile([P, PIECE], F32, name="picked_kb%d" % j)
-            nc.vector.tensor_copy(picked[:], kb_row[:].indirect(listed[j]))
+            nc.scalar.activation(picked[:], kb_row[:].indirect(listed[j]), COPY)
             picked_kb.append(picked)
 
         q_codes = keep.tile([P, NQ], U32, name="q_codes", tag="kb_then_codes", align_bytes=64)
@@ -89,7 +97,11 @@ def tile_attend_logprob_topk_kernel(tc, qT, k_words, k_scales, kb, ls, offs, out
             for c in range(PIECE // P):
                 nc.tensor.transpose(turned[:, c, :], picked_kb[j][:, c * P : (c + 1) * P], ident[:])
             col = keep.tile([P, PIECE // P], F32, name="kb_col%d" % j)
-            nc.scalar.copy(col[:], turned[:, :, KB_ROW])
+            pair = keep.tile([P, PIECE // P, 2], F32, name="kb_pair%d" % j)
+            for c in range(PIECE // P):
+                nc.scalar.activation(
+                    pair[:, c, :], turned[:, c, KB_ROWS[1] : P : P // 2], COPY, accum_out=col[:, c : c + 1]
+                )
             spread = psum.tile([P, PIECE], F32, name="spread%d" % j)
             for c in range(PIECE // P):
                 nc.tensor.transpose(spread[:, c * P : (c + 1) * P], col[:, c : c + 1].to_broadcast([P, P]), ident[:])
@@ -103,22 +115,36 @@ def tile_attend_logprob_topk_kernel(tc, qT, k_words, k_scales, kb, ls, offs, out
             nc.vector.tensor_copy(codes[:], words[:].bitcast(U32).indirect(listed[j]))
             k_codes.append(codes)
 
-        for j in range(N // PIECE):
-            cols = slice(j * PIECE, (j + 1) * PIECE)
-            for h in range(NQ // P):
-                rows = slice(h * P, (h + 1) * P)
-                acc = psum.tile([P, PIECE], F32, name="acc%d%d" % (h, j))
-                nc.tensor.matmul_mx(
-                    acc[:],
-                    lhsT=q_codes[:, rows].bitcast(FP8X4),
-                    lhsT_scale=q_plane[:, rows],
-                    rhs=k_codes[j][:].bitcast(FP8X4),
-                    rhs_scale=k_plane[:, cols],
-                    start=True,
-                    stop=True,
+        results = [[keep.tile([P, PIECE], F32, name="res%d%d" % (j, h)) for h in range(2)] for j in range(2)]
+        pieces = [
+            (0, 0, 0, P, "turned", P),
+            (0, 0, P, P, "acc1", P),
+            (0, 1, 0, PIECE, "acc2", PIECE),
+            (1, 1, 0, P, "acc3", 0),
+            (1, 1, P, P, "spread0", PIECE),
+            (1, 0, 0, P, "acc4", P),
+            (1, 0, P, P, "ls_turned", P),
+        ]
+        for n, (j, h, first, width, bank, stored) in enumerate(pieces):
+            rows = slice(h * P, (h + 1) * P)
+            part = slice(first, first + width)
+            cols = slice(j * PIECE + first, j * PIECE + first + width)
+            acc = psum.tile([P, width], F32, name="acc%d" % n, tag=bank)
+            nc.tensor.matmul_mx(
+                acc[:],
+                lhsT=q_codes[:, rows].bitcast(FP8X4),
+                lhsT_scale=q_plane[:, rows],
+                rhs=k_codes[j][:, part].bitcast(FP8X4),
+                rhs_scale=k_plane[:, cols],
+                start=True,
+                stop=True,
+            )
+            res = results[j][h]
+            nc.vector.scalar_tensor_tensor(
+                res[:, part], acc[:], ls_col[:, h : h + 1], kb_all[j][:, part], ALU.subtract, ALU.add
+            )
+            if stored:
+                last = first + width
+                nc.sync.dma_start(
+                    out[0, rows, j * PIECE + last - stored : j * PIECE + last], res[:, last - stored : last]
                 )
-                res = keep.tile([P, PIECE], F32, name="res%d%d" % (h, j))
-                nc.vector.scalar_tensor_tensor(
-                    res[:], acc[:], ls_col[:, h : h + 1], kb_all[j][:], ALU.subtract, ALU.add
-                )
-                nc.sync.dma_start(out[0, rows, cols], res[:])

@@ -17,8 +17,9 @@ P = 128
 T, N, D, NQ = 4096, 512, 512, 256
 PACK = 4
 PIECE = 256
-KB_ROWS = (P - 1, P // 2 - 1)
-HALF = T // 2
+KB_ROW = P - 1
+SCALAR_QUERIES = 80
+HEAD = 448
 
 FLOPS = 2 * NQ * D * N
 BYTES = P * T * 4 + 16 * T + D * NQ * 4 + T * 4 + NQ * 4 + P * (N // 16) * 2 + NQ * N * 4
@@ -32,53 +33,54 @@ def tile_attend_logprob_topk_kernel(tc, qT, k_words, k_scales, kb, ls, offs, out
 
         offsets = keep.tile([P, N // 16], U16, name="offsets")
         words = keep.tile([P, T], I32, name="words", align_bytes=64)
-        ls_col = keep.tile([P, NQ // P], F32, name="ls_col")
-        scale_rows = keep.tile([P, T], U8, name="scale_rows", align_bytes=64)
+        scale_rows = keep.tile([P, T], U8, name="scale_rows", tag="queries_then_late", align_bytes=64)
         kb_row = keep.tile([P, T], F32, name="kb_row", tag="kb_then_codes", align_bytes=64)
         k_plane = keep.tile([P, N], U8, name="k_plane", align_bytes=64)
         ident = keep.tile([P, P], F32, name="ident")
-        q_raw = keep.tile([P, PACK, NQ], F32, name="q_raw")
+        q_raw0 = keep.tile([P, PACK, P], F32, name="q_raw0")
 
         scale_words = scale_rows[:].bitcast(I32)
         nc.vector.memset(scale_words[:, 0:255], 0)
         nc.vector.memset(scale_words[:, 255:512], 0)
         nc.gpsimd.memset(ident[:], 0.0)
         nc.gpsimd.memset(scale_words[:, 512:1024], 0)
-        nc.vector.memset(kb_row[0 : KB_ROWS[0], 0:1023], 0.0)
-        nc.vector.memset(kb_row[0 : KB_ROWS[0], 1023:HALF], 0.0)
-        nc.vector.memset(kb_row[0 : KB_ROWS[1], HALF : HALF + 575], 0.0)
-        nc.vector.memset(kb_row[0 : KB_ROWS[1], HALF + 575 : HALF + 1152], 0.0)
+        nc.vector.memset(kb_row[0:KB_ROW, 0:959], 0.0)
+        nc.vector.memset(kb_row[0:KB_ROW, 959:1920], 0.0)
         ls_rows = keep.tile([P, P], F32, name="ls_rows")
-        nc.gpsimd.memset(ls_rows[0 : P - 2, :], 0.0)
         make_identity(nc, ident[:], nomemset=True)
-        nc.gpsimd.memset(kb_row[0 : KB_ROWS[1], HALF + 1152 : T], 0.0)
-        nc.gpsimd.memset(kb_row[P // 2 : P, HALF:T], 0.0)
+        nc.gpsimd.memset(kb_row[0:KB_ROW, 1920:T], 0.0)
+        nc.gpsimd.memset(k_plane[:].bitcast(I32), 0)
+        nc.gpsimd.memset(ls_rows[0 : P - 2, :], 0.0)
 
         words_hbm = k_words[0].rearrange("p n t -> p (n t)").bitcast(I32)
-        nc.sync.dma_start(q_raw[:], qT[0].rearrange("(p t) q -> p t q", t=PACK))
-        nc.sync.dma_start(ls_rows[P - 2 : P, :], ls[0].rearrange("(h p) o -> h (p o)", p=P))
+        q_hbm = qT[0].rearrange("(p t) q -> p t q", t=PACK)
+        nc.sync.dma_start(q_raw0[:], q_hbm[:, :, 0:P])
+        nc.sync.dma_start(words[:, 0:HEAD], words_hbm[:, 0:HEAD])
         nc.sync.dma_start(offsets[:], offs)
         nc.sync.dma_start(scale_rows[0:P:8, :].bitcast(I32), k_scales[0].bitcast(I32))
-        for half, row in enumerate(KB_ROWS):
-            stretch = slice(half * HALF, (half + 1) * HALF)
-            nc.sync.dma_start(kb_row[row : row + 1, stretch], kb[0:1, stretch])
-        nc.sync.dma_start(words[:], words_hbm)
+        nc.sync.dma_start(kb_row[KB_ROW:P, :], kb[0:1, :])
+        nc.sync.dma_start(words[:, HEAD:T], words_hbm[:, HEAD:T])
+        nc.sync.dma_start(ls_rows[P - 2 : P, :], ls[0].rearrange("(h p) o -> h (p o)", p=P))
 
-        ls_turned = psum.tile([P, P], F32, name="ls_turned")
-        nc.tensor.transpose(ls_turned[:], ls_rows[:], ident[:])
-        nc.scalar.copy(ls_col[:], ls_turned[:, P - 2 : P])
+        q_codes = []
+        q_plane = [keep.tile([P, P], U8, name="q_plane%d" % h, align_bytes=64) for h in range(2)]
+        q_bf = [
+            keep.tile([P, P, PACK], BF16, name="q_bf0", tag="q_bf0", align_bytes=64),
+            keep.tile([P, P, PACK], BF16, name="q_bf1", align_bytes=64),
+        ]
 
-        q_bf = keep.tile([P, NQ, PACK], BF16, name="q_bf", align_bytes=64)
-        nc.scalar.copy(
-            q_bf[:].rearrange("p (c i) t -> p c t i", i=4),
-            q_raw[:].rearrange("p t (c i) -> p c t i", i=4),
-        )
+        def cast_on_scalar(h, raw, count):
+            nc.scalar.copy(
+                q_bf[h][:, 0:count, :].rearrange("p (c i) t -> p c t i", i=4),
+                raw[:, :, 0:count].rearrange("p t (c i) -> p c t i", i=4),
+            )
 
-        picked_scales = keep.tile([P, N], U8, name="picked_scales", align_bytes=64)
-        nc.vector.tensor_copy(picked_scales[:], scale_rows[:].indirect(offsets[:]))
-        nc.vector.tensor_copy(k_plane[:].bitcast(I32), picked_scales[:].bitcast(I32))
-        for r in range(1, 4):
-            nc.sync.dma_start(k_plane[r:P:32, :].bitcast(I32), picked_scales[8 * r : P : 32, :].bitcast(I32))
+        def quantise_queries(h):
+            tag = "kb_then_codes" if h == 0 else "q_codes1"
+            q_codes.append(keep.tile([P, P], U32, name="q_codes%d" % h, tag=tag, align_bytes=64))
+            nc.vector.quantize_mx(q_codes[h][:].bitcast(FP8X4), q_plane[h][:], q_bf[h][:].rearrange("p q t -> p (q t)"))
+
+        cast_on_scalar(0, q_raw0, P)
 
         listed = [offsets[:, j * PIECE // 16 : (j + 1) * PIECE // 16] for j in range(N // PIECE)]
         picked_kb = []
@@ -87,21 +89,22 @@ def tile_attend_logprob_topk_kernel(tc, qT, k_words, k_scales, kb, ls, offs, out
             nc.scalar.activation(picked[:], kb_row[:].indirect(listed[j]), COPY)
             picked_kb.append(picked)
 
-        q_codes = keep.tile([P, NQ], U32, name="q_codes", tag="kb_then_codes", align_bytes=64)
-        q_plane = keep.tile([P, NQ], U8, name="q_plane", align_bytes=64)
-        nc.vector.quantize_mx(q_codes[:].bitcast(FP8X4), q_plane[:], q_bf[:].rearrange("p q t -> p (q t)"))
+        picked_scales = keep.tile([P, N], U8, name="picked_scales", align_bytes=64)
+        nc.vector.tensor_copy(picked_scales[:], scale_rows[:].indirect(offsets[:]))
+        for r in range(4):
+            nc.sync.dma_start(k_plane[r:P:32, :].bitcast(I32), picked_scales[8 * r : P : 32, :].bitcast(I32))
+        q_raw1 = keep.tile([P, PACK, P], F32, name="q_raw1", tag="queries_then_late", align_bytes=64)
+        nc.sync.dma_start(q_raw1[:], q_hbm[:, :, P:NQ])
+
+        quantise_queries(0)
 
         kb_all = []
         for j in range(N // PIECE):
-            turned = psum.tile([P, PIECE // P, P], F32, name="turned%d" % j, tag="ls_turned" if j else "turned")
+            turned = psum.tile([P, PIECE // P, P], F32, name="turned%d" % j, tag="turned%d" % j)
             for c in range(PIECE // P):
                 nc.tensor.transpose(turned[:, c, :], picked_kb[j][:, c * P : (c + 1) * P], ident[:])
             col = keep.tile([P, PIECE // P], F32, name="kb_col%d" % j)
-            pair = keep.tile([P, PIECE // P, 2], F32, name="kb_pair%d" % j)
-            for c in range(PIECE // P):
-                nc.scalar.activation(
-                    pair[:, c, :], turned[:, c, KB_ROWS[1] : P : P // 2], COPY, accum_out=col[:, c : c + 1]
-                )
+            nc.scalar.copy(col[:], turned[:, :, KB_ROW])
             spread = psum.tile([P, PIECE], F32, name="spread%d" % j)
             for c in range(PIECE // P):
                 nc.tensor.transpose(spread[:, c * P : (c + 1) * P], col[:, c : c + 1].to_broadcast([P, P]), ident[:])
@@ -109,42 +112,44 @@ def tile_attend_logprob_topk_kernel(tc, qT, k_words, k_scales, kb, ls, offs, out
             nc.scalar.copy(spread_sb[:], spread[:])
             kb_all.append(spread_sb)
 
+        ls_turned = psum.tile([P, P], F32, name="ls_turned", tag="turned0")
+        nc.tensor.transpose(ls_turned[:], ls_rows[:], ident[:])
+
         k_codes = []
         for j in range(N // PIECE):
             codes = keep.tile([P, PIECE], U32, name="k_codes%d" % j, align_bytes=64)
             nc.vector.tensor_copy(codes[:], words[:].bitcast(U32).indirect(listed[j]))
             k_codes.append(codes)
 
-        results = [[keep.tile([P, PIECE], F32, name="res%d%d" % (j, h)) for h in range(2)] for j in range(2)]
-        pieces = [
-            (0, 0, 0, P, "turned", P),
-            (0, 0, P, P, "acc1", P),
-            (0, 1, 0, PIECE, "acc2", PIECE),
-            (1, 1, 0, P, "acc3", 0),
-            (1, 1, P, P, "spread0", PIECE),
-            (1, 0, 0, P, "acc4", P),
-            (1, 0, P, P, "ls_turned", P),
-        ]
-        for n, (j, h, first, width, bank, stored) in enumerate(pieces):
+        cast_on_scalar(1, q_raw1, SCALAR_QUERIES)
+        nc.gpsimd.tensor_scalar(
+            q_bf[1][:, SCALAR_QUERIES:P, :],
+            q_raw1[:, :, SCALAR_QUERIES:P].rearrange("p t q -> p q t"),
+            1.0,
+            0.0,
+            ALU.mult,
+            ALU.add,
+        )
+        quantise_queries(1)
+        ls_col = keep.tile([P, NQ // P], F32, name="ls_col", tag="queries_then_late", align_bytes=64)
+        nc.scalar.copy(ls_col[:], ls_turned[:, P - 2 : P])
+
+        for h in range(NQ // P):
             rows = slice(h * P, (h + 1) * P)
-            part = slice(first, first + width)
-            cols = slice(j * PIECE + first, j * PIECE + first + width)
-            acc = psum.tile([P, width], F32, name="acc%d" % n, tag=bank)
-            nc.tensor.matmul_mx(
-                acc[:],
-                lhsT=q_codes[:, rows].bitcast(FP8X4),
-                lhsT_scale=q_plane[:, rows],
-                rhs=k_codes[j][:, part].bitcast(FP8X4),
-                rhs_scale=k_plane[:, cols],
-                start=True,
-                stop=True,
-            )
-            res = results[j][h]
-            nc.vector.scalar_tensor_tensor(
-                res[:, part], acc[:], ls_col[:, h : h + 1], kb_all[j][:, part], ALU.subtract, ALU.add
-            )
-            if stored:
-                last = first + width
-                nc.sync.dma_start(
-                    out[0, rows, j * PIECE + last - stored : j * PIECE + last], res[:, last - stored : last]
+            res = keep.tile([P, N], F32, name="res%d" % h)
+            for j in range(N // PIECE):
+                cols = slice(j * PIECE, (j + 1) * PIECE)
+                acc = psum.tile([P, PIECE], F32, name="acc%d%d" % (h, j))
+                nc.tensor.matmul_mx(
+                    acc[:],
+                    lhsT=q_codes[h][:].bitcast(FP8X4),
+                    lhsT_scale=q_plane[h][:],
+                    rhs=k_codes[j][:].bitcast(FP8X4),
+                    rhs_scale=k_plane[:, cols],
+                    start=True,
+                    stop=True,
                 )
+                nc.vector.scalar_tensor_tensor(
+                    res[:, cols], acc[:], ls_col[:, h : h + 1], kb_all[j][:], ALU.subtract, ALU.add
+                )
+                nc.sync.dma_start(out[0, rows, cols], res[:, cols])

from contextlib import ExitStack

import concourse.mybir as mybir
from concourse.masks import make_identity

F32 = mybir.dt.float32
BF16 = mybir.dt.bfloat16
I32 = mybir.dt.int32
U32 = mybir.dt.uint32
U16 = mybir.dt.uint16
U8 = mybir.dt.uint8
FP8X4 = mybir.dt.float8_e4m3fn_x4
ALU = mybir.AluOpType
COPY = mybir.ActivationFunctionType.Copy

P = 128
T, N, D, NQ = 4096, 512, 512, 256
PACK = 4
PIECE = 256
KB_ROW = P - 1
SCALAR_QUERIES = 80
HEAD = 448

FLOPS = 2 * NQ * D * N
BYTES = P * T * 4 + 16 * T + D * NQ * 4 + T * 4 + NQ * 4 + P * (N // 16) * 2 + NQ * N * 4


def tile_attend_logprob_topk_kernel(tc, qT, k_words, k_scales, kb, ls, offs, out):
    nc = tc.nc
    with ExitStack() as ctx:
        keep = ctx.enter_context(tc.tile_pool(name="keep", bufs=1))
        psum = ctx.enter_context(tc.psum_pool(name="psum", bufs=1))

        offsets = keep.tile([P, N // 16], U16, name="offsets")
        words = keep.tile([P, T], I32, name="words", align_bytes=64)
        scale_rows = keep.tile([P, T], U8, name="scale_rows", tag="queries_then_late", align_bytes=64)
        kb_row = keep.tile([P, T], F32, name="kb_row", tag="kb_then_codes", align_bytes=64)
        k_plane = keep.tile([P, N], U8, name="k_plane", align_bytes=64)
        ident = keep.tile([P, P], F32, name="ident")
        q_raw0 = keep.tile([P, PACK, P], F32, name="q_raw0")

        scale_words = scale_rows[:].bitcast(I32)
        nc.vector.memset(scale_words[:, 0:255], 0)
        nc.vector.memset(scale_words[:, 255:512], 0)
        nc.gpsimd.memset(ident[:], 0.0)
        nc.gpsimd.memset(scale_words[:, 512:1024], 0)
        nc.vector.memset(kb_row[0:KB_ROW, 0:959], 0.0)
        nc.vector.memset(kb_row[0:KB_ROW, 959:1920], 0.0)
        ls_rows = keep.tile([P, P], F32, name="ls_rows")
        make_identity(nc, ident[:], nomemset=True)
        nc.gpsimd.memset(kb_row[0:KB_ROW, 1920:T], 0.0)
        nc.gpsimd.memset(k_plane[:].bitcast(I32), 0)
        nc.gpsimd.memset(ls_rows[0 : P - 2, :], 0.0)

        words_hbm = k_words[0].rearrange("p n t -> p (n t)").bitcast(I32)
        q_hbm = qT[0].rearrange("(p t) q -> p t q", t=PACK)
        nc.sync.dma_start(q_raw0[:], q_hbm[:, :, 0:P])
        nc.sync.dma_start(words[:, 0:HEAD], words_hbm[:, 0:HEAD])
        nc.sync.dma_start(offsets[:], offs)
        nc.sync.dma_start(scale_rows[0:P:8, :].bitcast(I32), k_scales[0].bitcast(I32))
        nc.sync.dma_start(kb_row[KB_ROW:P, :], kb[0:1, :])
        nc.sync.dma_start(words[:, HEAD:T], words_hbm[:, HEAD:T])
        nc.sync.dma_start(ls_rows[P - 2 : P, :], ls[0].rearrange("(h p) o -> h (p o)", p=P))

        q_codes = []
        q_plane = [keep.tile([P, P], U8, name="q_plane%d" % h, align_bytes=64) for h in range(2)]
        q_bf = [
            keep.tile([P, P, PACK], BF16, name="q_bf0", tag="q_bf0", align_bytes=64),
            keep.tile([P, P, PACK], BF16, name="q_bf1", align_bytes=64),
        ]

        def cast_on_scalar(h, raw, count):
            nc.scalar.copy(
                q_bf[h][:, 0:count, :].rearrange("p (c i) t -> p c t i", i=4),
                raw[:, :, 0:count].rearrange("p t (c i) -> p c t i", i=4),
            )

        def quantise_queries(h):
            tag = "kb_then_codes" if h == 0 else "q_codes1"
            q_codes.append(keep.tile([P, P], U32, name="q_codes%d" % h, tag=tag, align_bytes=64))
            nc.vector.quantize_mx(q_codes[h][:].bitcast(FP8X4), q_plane[h][:], q_bf[h][:].rearrange("p q t -> p (q t)"))

        cast_on_scalar(0, q_raw0, P)

        listed = [offsets[:, j * PIECE // 16 : (j + 1) * PIECE // 16] for j in range(N // PIECE)]
        picked_kb = []
        for j in range(N // PIECE):
            picked = keep.tile([P, PIECE], F32, name="picked_kb%d" % j)
            nc.scalar.activation(picked[:], kb_row[:].indirect(listed[j]), COPY)
            picked_kb.append(picked)

        picked_scales = keep.tile([P, N], U8, name="picked_scales", align_bytes=64)
        nc.vector.tensor_copy(picked_scales[:], scale_rows[:].indirect(offsets[:]))
        for r in range(4):
            nc.sync.dma_start(k_plane[r:P:32, :].bitcast(I32), picked_scales[8 * r : P : 32, :].bitcast(I32))
        q_raw1 = keep.tile([P, PACK, P], F32, name="q_raw1", tag="queries_then_late", align_bytes=64)
        nc.sync.dma_start(q_raw1[:], q_hbm[:, :, P:NQ])

        quantise_queries(0)

        kb_all = []
        for j in range(N // PIECE):
            turned = psum.tile([P, PIECE // P, P], F32, name="turned%d" % j, tag="turned%d" % j)
            for c in range(PIECE // P):
                nc.tensor.transpose(turned[:, c, :], picked_kb[j][:, c * P : (c + 1) * P], ident[:])
            col = keep.tile([P, PIECE // P], F32, name="kb_col%d" % j)
            nc.scalar.copy(col[:], turned[:, :, KB_ROW])
            spread = psum.tile([P, PIECE], F32, name="spread%d" % j)
            for c in range(PIECE // P):
                nc.tensor.transpose(spread[:, c * P : (c + 1) * P], col[:, c : c + 1].to_broadcast([P, P]), ident[:])
            spread_sb = keep.tile([P, PIECE], F32, name="kb_all%d" % j)
            nc.scalar.copy(spread_sb[:], spread[:])
            kb_all.append(spread_sb)

        ls_turned = psum.tile([P, P], F32, name="ls_turned", tag="turned0")
        nc.tensor.transpose(ls_turned[:], ls_rows[:], ident[:])

        k_codes = []
        for j in range(N // PIECE):
            codes = keep.tile([P, PIECE], U32, name="k_codes%d" % j, align_bytes=64)
            nc.vector.tensor_copy(codes[:], words[:].bitcast(U32).indirect(listed[j]))
            k_codes.append(codes)

        cast_on_scalar(1, q_raw1, SCALAR_QUERIES)
        nc.gpsimd.tensor_scalar(
            q_bf[1][:, SCALAR_QUERIES:P, :],
            q_raw1[:, :, SCALAR_QUERIES:P].rearrange("p t q -> p q t"),
            1.0,
            0.0,
            ALU.mult,
            ALU.add,
        )
        quantise_queries(1)
        ls_col = keep.tile([P, NQ // P], F32, name="ls_col", tag="queries_then_late", align_bytes=64)
        nc.scalar.copy(ls_col[:], ls_turned[:, P - 2 : P])

        for h in range(NQ // P):
            rows = slice(h * P, (h + 1) * P)
            res = keep.tile([P, N], F32, name="res%d" % h)
            for j in range(N // PIECE):
                cols = slice(j * PIECE, (j + 1) * PIECE)
                acc = psum.tile([P, PIECE], F32, name="acc%d%d" % (h, j))
                nc.tensor.matmul_mx(
                    acc[:],
                    lhsT=q_codes[h][:].bitcast(FP8X4),
                    lhsT_scale=q_plane[h][:],
                    rhs=k_codes[j][:].bitcast(FP8X4),
                    rhs_scale=k_plane[:, cols],
                    start=True,
                    stop=True,
                )
                nc.vector.scalar_tensor_tensor(
                    res[:, cols], acc[:], ls_col[:, h : h + 1], kb_all[j][:], ALU.subtract, ALU.add
                )
                nc.sync.dma_start(out[0, rows, cols], res[:, cols])
